import numpy as np, ml_dtypes
CORES = [24,48,72,152,176,200]
N = 6
W, KW, DIL = 512, 5, 1
H = (KW // 2) * DIL
def setup_inputs(rng):
    return {"x": rng.standard_normal((N, 128, W), dtype=np.float32).astype(ml_dtypes.bfloat16), "w": rng.standard_normal((N, 128, KW * 128), dtype=np.float32).astype(ml_dtypes.bfloat16)}
def setup_inputs_big(rng):
    d = setup_inputs(rng)
    for k in ("x", "w"): d[k] = (d[k].astype(np.float32) * 1024.0).astype(d[k].dtype)
    return d
def setup_inputs_small(rng):
    d = setup_inputs(rng)
    for k in ("x", "w"): d[k] = (d[k].astype(np.float32) * (1 / 1024.0)).astype(d[k].dtype)
    return d
def reference(x, w):
    X, W_ = x.astype(np.float64), w.astype(np.float64)
    g = np.concatenate(list(X), axis=1)
    p = np.concatenate([g[:, -H:], g, g[:, :H]], axis=1)
    y = np.zeros((N, 128, W))
    for r in range(N):
        for i in range(KW):
            y[r] += W_[r][:, 128 * i:128 * i + 128].T @ p[:, W * r + i * DIL:W * r + i * DIL + W]
    return {"y": y.astype(ml_dtypes.bfloat16 if x.dtype != np.float64 else np.float64)}

from concourse.bass import DstId, RemoteDMATransfer

W, KW, C = 512, 5, 128
H = KW // 2
NB = 128
NA = W - 2 * H - NB

SCRATCH = {
    "edge": ("dram", [2, C, H], "bfloat16"),
    "xs": ("sbuf", [C, W + 2 * H], "bfloat16"),
    "ws": ("sbuf", [C, KW * C], "bfloat16"),
    "ya": ("sbuf", [C, NA], "bfloat16"),
    "yb": ("sbuf", [C, NB], "bfloat16"),
    "y0": ("sbuf", [C, H], "bfloat16"),
    "y1": ("sbuf", [C, H], "bfloat16"),
    "pa": ("psum", [C, 512], "float32"),
    "pb": ("psum", [C, 512], "float32"),
    "p0": ("psum", [C, 512], "float32"),
    "p1": ("psum", [C, 512], "float32"),
}
SEMAPHORES = ["e0", "e1", "ld", "in0", "in1", "h0", "h1", "sent",
              "ma", "mb", "m0", "m1", "ca", "cb", "c0", "c1", "st"]


def _chip_cores(c, topo):
    n = topo.CORES_PER_CHIP
    return [h for h in range(max(0, c - n), c + n) if topo.host(h) == topo.host(c) and topo.chip(h) == topo.chip(c)]


def _routes(T, topo):
    routes, n = [], len(T.cores)
    for r, c in enumerate(T.cores):
        for side, step in ((0, -1), (1, 1)):
            dst, relay = T.cores[(r + step) % n], None
            if not topo.may_write(c, dst):
                cands = [h for h in _chip_cores(c, topo)
                         if T.rank_of(h) is None and topo.may_write(h, dst) and topo.may_write(c, h)]
                cands.sort(key=lambda h: (topo.die(h) != topo.die(c), h))
                relay = cands[side % len(cands)]
            routes.append((c, side, relay, dst))
    return routes


def _engines(mask, n, skip=0):
    bits = [b for b in range(16) if (mask >> b) & 1][skip:skip + n]
    return sum(1 << b for b in bits)


def _count(mask):
    return sum((mask >> b) & 1 for b in range(16))


def _deliver(g, T, topo, src, side, dst):
    rid, pid = topo.addr(dst, src)
    m = topo.mask(src, dst)
    halo = 1 - side
    col = 0 if halo == 0 else H + W
    g.remote_dma(T.xs[:, col:col + H], T.edge[side], T.sem["h%d" % halo], T.sem.sent, pid, rid, m)
    return _count(m)


def rank_program(g, core, T, topo):
    routes = _routes(T, topo)

    if T.rank_of(core) is None:
        sent = 0
        for (src, side, relay, dst) in routes:
            if relay == core:
                g.wait_ge(T.sem["in%d" % side], 1)
                sent += _deliver(g, T, topo, core, side, dst)
        if sent:
            g.wait_ge(T.sem.sent, sent)
        return

    g.scalar.dma_start(T.edge[0], T.x[:, 0:H]).then_inc(T.sem.e0, 16)
    g.sync.dma_start(T.edge[1], T.x[:, W - H:W]).then_inc(T.sem.e1, 16)
    g.sync.dma_start(T.xs[:, H:H + W], T.x[:]).then_inc(T.sem.ld, 16)
    g.scalar.dma_start(T.ws[:], T.w[:]).then_inc(T.sem.ld, 16)

    mine = [rt for rt in routes if rt[0] == core]
    relayed = [rt for rt in mine if rt[2] is not None]
    sent = 0
    transfers = []
    for n, (src, side, relay, dst) in enumerate(relayed):
        g.wait_ge(T.sem["e%d" % side], 16)
        rid, pid = topo.addr(relay, core)
        transfers.append(RemoteDMATransfer(dst_ids=[DstId(rid=rid, pnc=pid)],
                                           dma_engine_mask=_engines(topo.mask(core, relay), 1, n),
                                           remote_sem=T.sem["in%d" % side], src=T.edge[side], dst=T.edge[side]))
        sent += 1
    if transfers:
        g.remote_dma_fused(transfers, local_sem=T.sem.sent)
    for (src, side, relay, dst) in mine:
        if relay is None:
            g.wait_ge(T.sem["e%d" % side], 16)
            sent += _deliver(g, T, topo, core, side, dst)

    def tap(out, c0, n, i, start, stop):
        return g.tensor.matmul(out[:, 0:n], T.ws[:, C * i:C * (i + 1)], T.xs[:, c0 + i:c0 + i + n], start, stop)

    g.tensor.wait_ge(T.sem.ld, 32)
    for out, c0, n, sem in ((T.pa, H, NA, T.sem.ma), (T.pb, H + NA, NB, T.sem.mb)):
        for i in range(KW):
            mm = tap(out, c0, n, i, i == 0, i == KW - 1)
        mm.then_inc(sem, 1)
    own = {0: list(range(H, KW)), 1: list(range(0, KW - H))}
    late = {0: list(range(0, H)), 1: list(range(KW - H, KW))}
    col0 = {0: 0, 1: W - H}
    for halo in (0, 1):
        for k, i in enumerate(own[halo]):
            tap(T["p%d" % halo], col0[halo], H, i, k == 0, False)
    arriving = {1 - side: (src if relay is None else relay, relay is not None)
                for (src, side, relay, dst) in routes if dst == core}
    order = sorted((0, 1), key=lambda halo: arriving[halo][1])
    for halo in order:
        g.tensor.wait_ge(T.sem["h%d" % halo], _count(topo.mask(arriving[halo][0], core)))
        for i in late[halo]:
            mm = tap(T["p%d" % halo], col0[halo], H, i, False, i == late[halo][-1])
        mm.then_inc(T.sem["m%d" % halo], 1)

    g.vector.wait_ge(T.sem.ma, 1)
    g.vector.tensor_copy(T.ya[:], T.pa[:, 0:NA]).then_inc(T.sem.ca, 1)
    g.vector.wait_ge(T.sem.mb, 1)
    g.vector.tensor_copy(T.yb[:], T.pb[:, 0:NB]).then_inc(T.sem.cb, 1)
    for halo in order:
        g.vector.wait_ge(T.sem["m%d" % halo], 1)
        g.vector.tensor_copy(T["y%d" % halo][:], T["p%d" % halo][:, 0:H]).then_inc(T.sem["c%d" % halo], 1)

    g.sync.wait_ge(T.sem.ca, 1)
    g.sync.dma_start(T.y[:, H:H + NA], T.ya[:]).then_inc(T.sem.st, 16)
    g.scalar.wait_ge(T.sem.cb, 1)
    g.scalar.dma_start(T.y[:, H + NA:W - H], T.yb[:]).then_inc(T.sem.st, 16)
    for q, halo in zip((g.sync, g.scalar), order):
        q.wait_ge(T.sem["c%d" % halo], 1)
        q.dma_start(T.y[:, col0[halo]:col0[halo] + H], T["y%d" % halo][:]).then_inc(T.sem.st, 16)

    g.wait_ge(T.sem.sent, sent)
    g.wait_ge(T.sem.st, 64)
